import numpy as np, ml_dtypes
CORES = [242,247,114,119]
N = 4
import mx_ref
NC = 256
LR = np.float32(0.0435)
BF = ml_dtypes.bfloat16
def cut(t, i, w=512):
    return t[:, w * i:w * i + w]
def tile(rs):
    return np.stack(rs, axis=2).reshape(128, -1).astype(BF)
def pick(b):
    s = np.zeros((128, 128, 4), np.float32)
    s[np.arange(128), np.arange(128), b] = 1.0
    return mx_ref.quantize(s.reshape(128, 512).astype(BF))
def setup_inputs(rng):
    def f(*shape):
        return mx_ref.flush((rng.standard_normal(shape, dtype=np.float32) * np.exp2(rng.integers(-2, 3, shape[:-1] + (1,)))).astype(BF))
    return {"b": f(N, 128, N * 512), "w": f(N, 128, 512), "x": f(N, 128, 4 * NC)}
def setup_inputs_blocks(rng):
    d = setup_inputs(rng)
    for k in ("b", "w", "x"): d[k] = mx_ref.spread(d[k], rng, 2)
    return d
def setup_inputs_wide(rng):
    d = setup_inputs(rng)
    for k in ("b", "w", "x"): d[k] = mx_ref.flush((d[k].astype(np.float32) * np.exp2(rng.integers(-4, 5, (N, 1, 1))).astype(np.float32)).astype(BF))
    return d
def reference(b, w, x, own=None):
    S = [pick(t) for t in range(4)]
    h = np.zeros((N, 128, 512), BF)
    for c in range(N):
        for r in range(N):
            q = mx_ref.quantize(cut(b[r], c))
            P = [mx_ref.matmul(S[t], q) for t in range(4)]
            Z = P if r == 0 else [z + p for z, p in zip(Z, P)]
        h[c] = tile([w[c].astype(np.float32)[:, t::4] - Z[t] * LR for t in range(4)])
    use = h if own is None else own["h"]
    H = [mx_ref.quantize(use[j]) for j in range(N)]
    y = np.zeros((N, 128, N * NC), np.float32)
    for r in range(N):
        qx = mx_ref.quantize(x[r])
        for j in range(N):
            y[r][:, NC * j:NC * j + NC] = mx_ref.matmul(H[j], qx)
    return {"h": h, "y": y}

@@ -1,0 +1,197 @@
+from concourse.bass import DstId, RemoteDMATransfer
+from concourse.mybir import dt, AluOpType, ActivationFunctionType
+
+N = 4
+W = 128
+XC = 256
+BANK = 512
+LR = 0.0435
+
+SCRATCH = {
+    "bt": ("sbuf", [128, N * 512], "bfloat16"),
+    "wt": ("sbuf", [128, 512], "bfloat16"),
+    "xt": ("sbuf", [128, 1024], "bfloat16"),
+    "ht": ("sbuf", [128, 512], "bfloat16"),
+    "eye": ("sbuf", [128, 516], "bfloat16"),
+    "m": ("sbuf", [128, 4 * W], "float32"),
+    "yt": ("sbuf", [128, N * XC], "float32"),
+    "bq": ("sbuf", [128, N * W], "float8_e4m3fn_x4"),
+    "bs": ("sbuf", [128, N * W], "uint8"),
+    "sq": ("sbuf", [128, 4 * W], "float8_e4m3fn_x4"),
+    "ss": ("sbuf", [128, 4 * W], "uint8"),
+    "xq": ("sbuf", [128, XC], "float8_e4m3fn_x4"),
+    "xs": ("sbuf", [128, XC], "uint8"),
+    "hq": ("sbuf", [128, W], "float8_e4m3fn_x4"),
+    "hs": ("sbuf", [128, W], "uint8"),
+    "gq": ("sbuf", [128, N * W], "float8_e4m3fn_x4"),
+    "gs": ("sbuf", [128, N * W], "uint8"),
+    "aq": ("sbuf", [128, N * W], "float8_e4m3fn_x4"),
+    "as": ("sbuf", [128, N * W], "uint8"),
+    "z": ("psum", [128, 4 * BANK], "float32"),
+    "py": ("psum", [128, 4 * BANK], "float32"),
+}
+SEMAPHORES = (["fill", "eyed", "s_q", "off_q", "on_q", "own_q", "x_q", "h_q", "h_t", "w_l", "x_l",
+               "left_off", "left_on", "left_h", "st_sync", "st_scal"]
+              + ["b_l%d" % i for i in range(N)] + ["g%d" % i for i in range(N)] + ["a%d" % i for i in range(N)]
+              + ["z%d" % i for i in range(4)] + ["m%d" % i for i in range(4)]
+              + ["y%d" % i for i in range(6)] + ["c%d" % i for i in range(6)])
+
+
+def _bits(mask):
+    return [e for e in range(mask.bit_length()) if mask >> e & 1]
+
+
+def _mask(engines):
+    return sum(1 << e for e in engines)
+
+
+def rank_program(g, core, T, topo):
+    rank = T.rank_of(core)
+    if rank is None:
+        return
+    cores = list(T.cores)
+
+    def here(c):
+        return topo.host(c) == topo.host(core) and topo.chip(c) == topo.chip(core)
+
+    others = [r for r in range(N) if r != rank]
+    on = [r for r in others if here(cores[r])][0]
+    off = sorted([r for r in others if not here(cores[r])], key=lambda r: topo.die(cores[r]) != topo.die(core))
+
+    leave = _bits(topo.mask(core, cores[off[0]]))
+    stay = [e for e in _bits(topo.mask(core, cores[on])) if e not in leave]
+    half = len(leave) // 2
+    eng = {off[0]: leave[:half], off[1]: leave[half:], on: stay[::2]}
+
+    def write(dests, src, dst, sem, left):
+        ts = []
+        for d in dests:
+            rid, pid = topo.addr(cores[d], core)
+            ts.append(RemoteDMATransfer(dst_ids=[DstId(rid=rid, pnc=pid)], dma_engine_mask=_mask(eng[d]),
+                                        remote_sem=sem, src=src(d), dst=dst))
+        g.remote_dma_fused(ts, local_sem=left)
+        return sum(len(eng[d]) for d in dests)
+
+    def col(i, w=W):
+        return slice(w * i, w * i + w)
+
+    sem = T.sem
+    v, t, s, a = g.vector, g.tensor, g.sync, g.scalar
+    Copy = ActivationFunctionType.Copy
+
+    def load(q, r):
+        q.dma_start(T.bt[:, col(r, 512)], T.b[:, col(r, 512)]).then_inc(sem["b_l%d" % r], 16)
+
+    load(s, off[0])
+    load(a, off[1])
+    load(s, on)
+    load(a, rank)
+    s.dma_start(T.wt[:], T.w[:]).then_inc(sem.w_l, 16)
+
+    v.memset(T.eye[:], 0.0).then_inc(sem.fill, 1)
+    g.wait_ge(sem.fill, 1)
+    g.affine_select(T.eye[:, 3:515:4], T.eye[:, 3:515:4], [[-1, 128]], AluOpType.not_equal, 1.0, 0, 1).then_inc(sem.eyed, 1)
+    v.wait_ge(sem.eyed, 1)
+    for b in range(4):
+        v.quantize_mx(T.sq[:, col(b)], T.ss[:, col(b)], T.eye[:, 3 - b:515 - b]).then_inc(sem.s_q, 1)
+
+    for r, q in ((off[0], "off_q"), (off[1], "off_q"), (on, "on_q"), (rank, "own_q")):
+        v.wait_ge(sem["b_l%d" % r], 16)
+        v.quantize_mx(T.bq[:, col(r)], T.bs[:, col(r)], T.bt[:, col(r, 512)]).then_inc(sem[q], 1)
+
+    def b_codes(d):
+        return T.bq[:, col(d)].bitcast(dt.uint8)
+
+    def b_plane(d):
+        return T.bs[:, col(d)]
+
+    g_codes, g_plane, g_sem = T.gq[:, col(rank)].bitcast(dt.uint8), T.gs[:, col(rank)], sem["g%d" % rank]
+    g.wait_ge(sem.off_q, 2)
+    n_off = write(off, b_codes, g_codes, g_sem, sem.left_off)
+    n_off += write(off, b_plane, g_plane, g_sem, sem.left_off)
+    g.wait_ge(sem.on_q, 1)
+    n_on = write([on], b_codes, g_codes, g_sem, sem.left_on)
+    n_on += write([on], b_plane, g_plane, g_sem, sem.left_on)
+
+    s.wait_ge(sem.left_off, n_off)
+    s.dma_start(T.xt[:], T.x[:]).then_inc(sem.x_l, 16)
+
+    def arrived(r, kind):
+        n = len(eng[off[0]]) if r in off else len(eng[on])
+        t.wait_ge(sem["%s%d" % (kind, r)], 2 * n)
+
+    def pick_mm(b, codes, plane, r, start, stop):
+        return t.matmul_mx(T.z[:, BANK * b:BANK * b + W], T.sq[:, col(b)], T.ss[:, col(b)],
+                           codes[:, col(r)], plane[:, col(r)], start, stop)
+
+    t.wait_ge(sem.s_q, 4)
+    t.wait_ge(sem.own_q, 1)
+    for b in range(4):
+        pick_mm(b, T.bq, T.bs, rank, True, False)
+    arrived(on, "g")
+    for b in range(4):
+        pick_mm(b, T.gq, T.gs, on, False, False)
+    arrived(off[0], "g")
+    arrived(off[1], "g")
+    for b in range(4):
+        pick_mm(b, T.gq, T.gs, off[0], False, False)
+        pick_mm(b, T.gq, T.gs, off[1], False, True).then_inc(sem["z%d" % b], 1)
+
+    v.wait_ge(sem.w_l, 16)
+    for b in range(4):
+        a.wait_ge(sem["z%d" % b], 1)
+        a.activation(T.m[:, col(b)], T.z[:, BANK * b:BANK * b + W], Copy, scale=LR).then_inc(sem["m%d" % b], 1)
+        v.wait_ge(sem["m%d" % b], 1)
+        v.tensor_tensor(T.ht[:, b:512:4], T.wt[:, b:512:4], T.m[:, col(b)], AluOpType.subtract).then_inc(sem.h_t, 1)
+    v.wait_ge(sem.h_t, 4)
+    v.quantize_mx(T.hq[:], T.hs[:], T.ht[:]).then_inc(sem.h_q, 1)
+
+    g.wait_ge(sem.h_q, 1)
+    dests = off + [on]
+    a_codes, a_plane, a_sem = T.aq[:, col(rank)].bitcast(dt.uint8), T["as"][:, col(rank)], sem["a%d" % rank]
+    n_h = write(dests, lambda d: T.hq[:].bitcast(dt.uint8), a_codes, a_sem, sem.left_h)
+    n_h += write(dests, lambda d: T.hs[:], a_plane, a_sem, sem.left_h)
+    g.wait_ge(sem.left_on, n_on)
+
+    s.wait_ge(sem.h_t, 4)
+    s.wait_ge(sem.left_h, n_h)
+    s.dma_start(T.h[:], T.ht[:]).then_inc(sem.st_sync, 16)
+
+    v.wait_ge(sem.x_l, 16)
+    v.quantize_mx(T.xq[:], T.xs[:], T.xt[:]).then_inc(sem.x_q, 1)
+    HX = XC // 2
+    jobs = [(rank, 0, XC, (T.py, 0), "v"), (on, 0, XC, (T.py, 1), "v"),
+            (off[0], 0, HX, (T.py, 2), "v"), (off[0], HX, HX, (T.py, 3), "a"),
+            (off[1], 0, HX, (T.z, 0), "v"), (off[1], HX, HX, (T.z, 1), "a")]
+    t.wait_ge(sem.h_q, 1)
+    t.wait_ge(sem.x_q, 1)
+    seen = [rank]
+    for k, (j, c0, n, (bank, i), eng_name) in enumerate(jobs):
+        if j not in seen:
+            arrived(j, "a")
+            seen.append(j)
+        if j == rank:
+            hq, hs = T.hq[:], T.hs[:]
+        else:
+            hq, hs = T.aq[:, col(j)], T["as"][:, col(j)]
+        out = bank[:, BANK * i:BANK * i + n]
+        t.matmul_mx(out, hq, hs, T.xq[:, c0:c0 + n], T.xs[:, c0:c0 + n], True, True).then_inc(sem["y%d" % k], 1)
+        dst = T.yt[:, XC * j + c0:XC * j + c0 + n]
+        if eng_name == "v":
+            v.wait_ge(sem["y%d" % k], 1)
+            v.tensor_copy(dst, out).then_inc(sem["c%d" % k], 1)
+        else:
+            a.wait_ge(sem["y%d" % k], 1)
+            a.activation(dst, out, Copy).then_inc(sem["c%d" % k], 1)
+
+    def store(q, j, waits, st):
+        for k in waits:
+            q.wait_ge(sem["c%d" % k], 1)
+        q.dma_start(T.y[:, col(j, XC)], T.yt[:, col(j, XC)]).then_inc(st, 16)
+
+    store(s, rank, [0], sem.st_sync)
+    store(s, on, [1], sem.st_sync)
+    store(s, off[0], [2, 3], sem.st_sync)
+    store(a, off[1], [4, 5], sem.st_scal)
+    s.wait_ge(sem.st_sync, 64)
+    a.wait_ge(sem.st_scal, 16)

@@ -30,9 +30,9 @@ SCRATCH = {
     "z": ("psum", [128, 4 * BANK], "float32"),
     "py": ("psum", [128, 4 * BANK], "float32"),
 }
-SEMAPHORES = (["fill", "eyed", "s_q", "off_q", "on_q", "own_q", "x_q", "h_q", "h_t", "w_l", "x_l",
-               "left_off", "left_on", "left_h", "st_sync", "st_scal"]
-              + ["b_l%d" % i for i in range(N)] + ["g%d" % i for i in range(N)] + ["a%d" % i for i in range(N)]
+SEMAPHORES = (["fill", "eyed", "s_q", "x_q", "h_q", "h_t", "w_l", "x_l", "left_g", "left_h", "sent_h", "st_sync", "st_scal"]
+              + ["b_l%d" % i for i in range(N)] + ["b_q%d" % i for i in range(N)]
+              + ["g%d" % i for i in range(N)] + ["a%d" % i for i in range(N)]
               + ["z%d" % i for i in range(4)] + ["m%d" % i for i in range(4)]
               + ["y%d" % i for i in range(6)] + ["c%d" % i for i in range(6)])
 
@@ -56,12 +56,11 @@ def rank_program(g, core, T, topo):
 
     others = [r for r in range(N) if r != rank]
     on = [r for r in others if here(cores[r])][0]
-    off = sorted([r for r in others if not here(cores[r])], key=lambda r: topo.die(cores[r]) != topo.die(core))
+    off = sorted([r for r in others if not here(cores[r])], key=lambda r: topo.die(cores[r]) == topo.die(core))
 
     leave = _bits(topo.mask(core, cores[off[0]]))
     stay = [e for e in _bits(topo.mask(core, cores[on])) if e not in leave]
-    half = len(leave) // 2
-    eng = {off[0]: leave[:half], off[1]: leave[half:], on: stay[::2]}
+    eng = {off[0]: leave, off[1]: leave, on: stay}
 
     def write(dests, src, dst, sem, left):
         ts = []
@@ -79,25 +78,30 @@ def rank_program(g, core, T, topo):
     v, t, s, a = g.vector, g.tensor, g.sync, g.scalar
     Copy = ActivationFunctionType.Copy
 
-    def load(q, r):
-        q.dma_start(T.bt[:, col(r, 512)], T.b[:, col(r, 512)]).then_inc(sem["b_l%d" % r], 16)
+    def load(q, r, p0=0, p1=128):
+        q.dma_start(T.bt[p0:p1, col(r, 512)], T.b[p0:p1, col(r, 512)]).then_inc(sem["b_l%d" % r], 16)
 
-    load(s, off[0])
-    load(a, off[1])
-    load(s, on)
-    load(a, rank)
-    s.dma_start(T.wt[:], T.w[:]).then_inc(sem.w_l, 16)
+    load(s, off[0], 0, 64)
+    load(a, off[0], 64, 128)
+    load(s, off[1])
+    load(a, on)
+    load(s, rank)
+    a.dma_start(T.wt[:], T.w[:]).then_inc(sem.w_l, 16)
 
     v.memset(T.eye[:], 0.0).then_inc(sem.fill, 1)
     g.wait_ge(sem.fill, 1)
     g.affine_select(T.eye[:, 3:515:4], T.eye[:, 3:515:4], [[-1, 128]], AluOpType.not_equal, 1.0, 0, 1).then_inc(sem.eyed, 1)
+
+    def pack(r):
+        v.wait_ge(sem["b_l%d" % r], 32 if r == off[0] else 16)
+        v.quantize_mx(T.bq[:, col(r)], T.bs[:, col(r)], T.bt[:, col(r, 512)]).then_inc(sem["b_q%d" % r], 1)
+
+    for r in off + [on]:
+        pack(r)
     v.wait_ge(sem.eyed, 1)
     for b in range(4):
         v.quantize_mx(T.sq[:, col(b)], T.ss[:, col(b)], T.eye[:, 3 - b:515 - b]).then_inc(sem.s_q, 1)
-
-    for r, q in ((off[0], "off_q"), (off[1], "off_q"), (on, "on_q"), (rank, "own_q")):
-        v.wait_ge(sem["b_l%d" % r], 16)
-        v.quantize_mx(T.bq[:, col(r)], T.bs[:, col(r)], T.bt[:, col(r, 512)]).then_inc(sem[q], 1)
+    pack(rank)
 
     def b_codes(d):
         return T.bq[:, col(d)].bitcast(dt.uint8)
@@ -106,55 +110,57 @@ def rank_program(g, core, T, topo):
         return T.bs[:, col(d)]
 
     g_codes, g_plane, g_sem = T.gq[:, col(rank)].bitcast(dt.uint8), T.gs[:, col(rank)], sem["g%d" % rank]
-    g.wait_ge(sem.off_q, 2)
-    n_off = write(off, b_codes, g_codes, g_sem, sem.left_off)
-    n_off += write(off, b_plane, g_plane, g_sem, sem.left_off)
-    g.wait_ge(sem.on_q, 1)
-    n_on = write([on], b_codes, g_codes, g_sem, sem.left_on)
-    n_on += write([on], b_plane, g_plane, g_sem, sem.left_on)
+    n_g = 0
+    for dests in ([off[0]], [off[1], on]):
+        for d in dests:
+            g.wait_ge(sem["b_q%d" % d], 1)
+        n_g += write(dests, b_codes, g_codes, g_sem, sem.left_g)
+        n_g += write(dests, b_plane, g_plane, g_sem, sem.left_g)
 
-    s.wait_ge(sem.left_off, n_off)
+    s.wait_ge(sem.left_g, n_g)
     s.dma_start(T.xt[:], T.x[:]).then_inc(sem.x_l, 16)
 
     def arrived(r, kind):
-        n = len(eng[off[0]]) if r in off else len(eng[on])
-        t.wait_ge(sem["%s%d" % (kind, r)], 2 * n)
-
-    def pick_mm(b, codes, plane, r, start, stop):
-        return t.matmul_mx(T.z[:, BANK * b:BANK * b + W], T.sq[:, col(b)], T.ss[:, col(b)],
-                           codes[:, col(r)], plane[:, col(r)], start, stop)
+        t.wait_ge(sem["%s%d" % (kind, r)], 2 * len(eng[r]))
 
     t.wait_ge(sem.s_q, 4)
-    t.wait_ge(sem.own_q, 1)
-    for b in range(4):
-        pick_mm(b, T.bq, T.bs, rank, True, False)
-    arrived(on, "g")
-    for b in range(4):
-        pick_mm(b, T.gq, T.gs, on, False, False)
-    arrived(off[0], "g")
-    arrived(off[1], "g")
-    for b in range(4):
-        pick_mm(b, T.gq, T.gs, off[0], False, False)
-        pick_mm(b, T.gq, T.gs, off[1], False, True).then_inc(sem["z%d" % b], 1)
+    t.wait_ge(sem["b_q%d" % rank], 1)
+    order = [rank, off[0], on, off[1]]
+    for r in order:
+        if r != rank:
+            arrived(r, "g")
+        codes, plane = (T.bq, T.bs) if r == rank else (T.gq, T.gs)
+        for b in range(4):
+            mm = t.matmul_mx(T.z[:, BANK * b:BANK * b + W], T.sq[:, col(b)], T.ss[:, col(b)],
+                             codes[:, col(r)], plane[:, col(r)], r == order[0], r == order[-1])
+            if r == order[-1]:
+                mm.then_inc(sem["z%d" % b], 1)
 
     v.wait_ge(sem.w_l, 16)
     for b in range(4):
-        a.wait_ge(sem["z%d" % b], 1)
-        a.activation(T.m[:, col(b)], T.z[:, BANK * b:BANK * b + W], Copy, scale=LR).then_inc(sem["m%d" % b], 1)
+        zb, mb = T.z[:, BANK * b:BANK * b + W], T.m[:, col(b)]
+        if b == 0:
+            v.wait_ge(sem["z%d" % b], 1)
+            v.tensor_scalar(mb, zb, LR, None, AluOpType.mult).then_inc(sem["m%d" % b], 1)
+        else:
+            a.wait_ge(sem["z%d" % b], 1)
+            a.activation(mb, zb, Copy, scale=LR).then_inc(sem["m%d" % b], 1)
         v.wait_ge(sem["m%d" % b], 1)
-        v.tensor_tensor(T.ht[:, b:512:4], T.wt[:, b:512:4], T.m[:, col(b)], AluOpType.subtract).then_inc(sem.h_t, 1)
+        v.tensor_tensor(T.ht[:, b:512:4], T.wt[:, b:512:4], mb, AluOpType.subtract).then_inc(sem.h_t, 1)
     v.wait_ge(sem.h_t, 4)
     v.quantize_mx(T.hq[:], T.hs[:], T.ht[:]).then_inc(sem.h_q, 1)
 
     g.wait_ge(sem.h_q, 1)
-    dests = off + [on]
     a_codes, a_plane, a_sem = T.aq[:, col(rank)].bitcast(dt.uint8), T["as"][:, col(rank)], sem["a%d" % rank]
-    n_h = write(dests, lambda d: T.hq[:].bitcast(dt.uint8), a_codes, a_sem, sem.left_h)
-    n_h += write(dests, lambda d: T.hs[:], a_plane, a_sem, sem.left_h)
-    g.wait_ge(sem.left_on, n_on)
+    n_h = 0
+    for dests in ([off[0], on], [off[1]]):
+        n_h += write(dests, lambda d: T.hq[:].bitcast(dt.uint8), a_codes, a_sem, sem.left_h)
+        n_h += write(dests, lambda d: T.hs[:], a_plane, a_sem, sem.left_h)
+    g.sem_inc(sem.sent_h, 1)
+    g.wait_ge(sem.left_h, n_h)
 
     s.wait_ge(sem.h_t, 4)
-    s.wait_ge(sem.left_h, n_h)
+    s.wait_ge(sem.sent_h, 1)
     s.dma_start(T.h[:], T.ht[:]).then_inc(sem.st_sync, 16)
 
     v.wait_ge(sem.x_l, 16)

from concourse.bass import DstId, RemoteDMATransfer
from concourse.mybir import dt, AluOpType, ActivationFunctionType

N = 4
W = 128
XC = 256
BANK = 512
LR = 0.0435

SCRATCH = {
    "bt": ("sbuf", [128, N * 512], "bfloat16"),
    "wt": ("sbuf", [128, 512], "bfloat16"),
    "xt": ("sbuf", [128, 1024], "bfloat16"),
    "ht": ("sbuf", [128, 512], "bfloat16"),
    "eye": ("sbuf", [128, 516], "bfloat16"),
    "m": ("sbuf", [128, 4 * W], "float32"),
    "yt": ("sbuf", [128, N * XC], "float32"),
    "bq": ("sbuf", [128, N * W], "float8_e4m3fn_x4"),
    "bs": ("sbuf", [128, N * W], "uint8"),
    "sq": ("sbuf", [128, 4 * W], "float8_e4m3fn_x4"),
    "ss": ("sbuf", [128, 4 * W], "uint8"),
    "xq": ("sbuf", [128, XC], "float8_e4m3fn_x4"),
    "xs": ("sbuf", [128, XC], "uint8"),
    "hq": ("sbuf", [128, W], "float8_e4m3fn_x4"),
    "hs": ("sbuf", [128, W], "uint8"),
    "gq": ("sbuf", [128, N * W], "float8_e4m3fn_x4"),
    "gs": ("sbuf", [128, N * W], "uint8"),
    "aq": ("sbuf", [128, N * W], "float8_e4m3fn_x4"),
    "as": ("sbuf", [128, N * W], "uint8"),
    "z": ("psum", [128, 4 * BANK], "float32"),
    "py": ("psum", [128, 4 * BANK], "float32"),
}
SEMAPHORES = (["fill", "eyed", "s_q", "x_q", "h_q", "h_t", "w_l", "x_l", "left_g", "left_h", "sent_h", "st_sync", "st_scal"]
              + ["b_l%d" % i for i in range(N)] + ["b_q%d" % i for i in range(N)]
              + ["g%d" % i for i in range(N)] + ["a%d" % i for i in range(N)]
              + ["z%d" % i for i in range(4)] + ["m%d" % i for i in range(4)]
              + ["y%d" % i for i in range(6)] + ["c%d" % i for i in range(6)])


def _bits(mask):
    return [e for e in range(mask.bit_length()) if mask >> e & 1]


def _mask(engines):
    return sum(1 << e for e in engines)


def rank_program(g, core, T, topo):
    rank = T.rank_of(core)
    if rank is None:
        return
    cores = list(T.cores)

    def here(c):
        return topo.host(c) == topo.host(core) and topo.chip(c) == topo.chip(core)

    others = [r for r in range(N) if r != rank]
    on = [r for r in others if here(cores[r])][0]
    off = sorted([r for r in others if not here(cores[r])], key=lambda r: topo.die(cores[r]) == topo.die(core))

    leave = _bits(topo.mask(core, cores[off[0]]))
    stay = [e for e in _bits(topo.mask(core, cores[on])) if e not in leave]
    eng = {off[0]: leave, off[1]: leave, on: stay}

    def write(dests, src, dst, sem, left):
        ts = []
        for d in dests:
            rid, pid = topo.addr(cores[d], core)
            ts.append(RemoteDMATransfer(dst_ids=[DstId(rid=rid, pnc=pid)], dma_engine_mask=_mask(eng[d]),
                                        remote_sem=sem, src=src(d), dst=dst))
        g.remote_dma_fused(ts, local_sem=left)
        return sum(len(eng[d]) for d in dests)

    def col(i, w=W):
        return slice(w * i, w * i + w)

    sem = T.sem
    v, t, s, a = g.vector, g.tensor, g.sync, g.scalar
    Copy = ActivationFunctionType.Copy

    def load(q, r, p0=0, p1=128):
        q.dma_start(T.bt[p0:p1, col(r, 512)], T.b[p0:p1, col(r, 512)]).then_inc(sem["b_l%d" % r], 16)

    load(s, off[0], 0, 64)
    load(a, off[0], 64, 128)
    load(s, off[1])
    load(a, on)
    load(s, rank)
    a.dma_start(T.wt[:], T.w[:]).then_inc(sem.w_l, 16)

    v.memset(T.eye[:], 0.0).then_inc(sem.fill, 1)
    g.wait_ge(sem.fill, 1)
    g.affine_select(T.eye[:, 3:515:4], T.eye[:, 3:515:4], [[-1, 128]], AluOpType.not_equal, 1.0, 0, 1).then_inc(sem.eyed, 1)

    def pack(r):
        v.wait_ge(sem["b_l%d" % r], 32 if r == off[0] else 16)
        v.quantize_mx(T.bq[:, col(r)], T.bs[:, col(r)], T.bt[:, col(r, 512)]).then_inc(sem["b_q%d" % r], 1)

    for r in off + [on]:
        pack(r)
    v.wait_ge(sem.eyed, 1)
    for b in range(4):
        v.quantize_mx(T.sq[:, col(b)], T.ss[:, col(b)], T.eye[:, 3 - b:515 - b]).then_inc(sem.s_q, 1)
    pack(rank)

    def b_codes(d):
        return T.bq[:, col(d)].bitcast(dt.uint8)

    def b_plane(d):
        return T.bs[:, col(d)]

    g_codes, g_plane, g_sem = T.gq[:, col(rank)].bitcast(dt.uint8), T.gs[:, col(rank)], sem["g%d" % rank]
    n_g = 0
    for dests in ([off[0]], [off[1], on]):
        for d in dests:
            g.wait_ge(sem["b_q%d" % d], 1)
        n_g += write(dests, b_codes, g_codes, g_sem, sem.left_g)
        n_g += write(dests, b_plane, g_plane, g_sem, sem.left_g)

    s.wait_ge(sem.left_g, n_g)
    s.dma_start(T.xt[:], T.x[:]).then_inc(sem.x_l, 16)

    def arrived(r, kind):
        t.wait_ge(sem["%s%d" % (kind, r)], 2 * len(eng[r]))

    t.wait_ge(sem.s_q, 4)
    t.wait_ge(sem["b_q%d" % rank], 1)
    order = [rank, off[0], on, off[1]]
    for r in order:
        if r != rank:
            arrived(r, "g")
        codes, plane = (T.bq, T.bs) if r == rank else (T.gq, T.gs)
        for b in range(4):
            mm = t.matmul_mx(T.z[:, BANK * b:BANK * b + W], T.sq[:, col(b)], T.ss[:, col(b)],
                             codes[:, col(r)], plane[:, col(r)], r == order[0], r == order[-1])
            if r == order[-1]:
                mm.then_inc(sem["z%d" % b], 1)

    v.wait_ge(sem.w_l, 16)
    for b in range(4):
        zb, mb = T.z[:, BANK * b:BANK * b + W], T.m[:, col(b)]
        if b == 0:
            v.wait_ge(sem["z%d" % b], 1)
            v.tensor_scalar(mb, zb, LR, None, AluOpType.mult).then_inc(sem["m%d" % b], 1)
        else:
            a.wait_ge(sem["z%d" % b], 1)
            a.activation(mb, zb, Copy, scale=LR).then_inc(sem["m%d" % b], 1)
        v.wait_ge(sem["m%d" % b], 1)
        v.tensor_tensor(T.ht[:, b:512:4], T.wt[:, b:512:4], mb, AluOpType.subtract).then_inc(sem.h_t, 1)
    v.wait_ge(sem.h_t, 4)
    v.quantize_mx(T.hq[:], T.hs[:], T.ht[:]).then_inc(sem.h_q, 1)

    g.wait_ge(sem.h_q, 1)
    a_codes, a_plane, a_sem = T.aq[:, col(rank)].bitcast(dt.uint8), T["as"][:, col(rank)], sem["a%d" % rank]
    n_h = 0
    for dests in ([off[0], on], [off[1]]):
        n_h += write(dests, lambda d: T.hq[:].bitcast(dt.uint8), a_codes, a_sem, sem.left_h)
        n_h += write(dests, lambda d: T.hs[:], a_plane, a_sem, sem.left_h)
    g.sem_inc(sem.sent_h, 1)
    g.wait_ge(sem.left_h, n_h)

    s.wait_ge(sem.h_t, 4)
    s.wait_ge(sem.sent_h, 1)
    s.dma_start(T.h[:], T.ht[:]).then_inc(sem.st_sync, 16)

    v.wait_ge(sem.x_l, 16)
    v.quantize_mx(T.xq[:], T.xs[:], T.xt[:]).then_inc(sem.x_q, 1)
    HX = XC // 2
    jobs = [(rank, 0, XC, (T.py, 0), "v"), (on, 0, XC, (T.py, 1), "v"),
            (off[0], 0, HX, (T.py, 2), "v"), (off[0], HX, HX, (T.py, 3), "a"),
            (off[1], 0, HX, (T.z, 0), "v"), (off[1], HX, HX, (T.z, 1), "a")]
    t.wait_ge(sem.h_q, 1)
    t.wait_ge(sem.x_q, 1)
    seen = [rank]
    for k, (j, c0, n, (bank, i), eng_name) in enumerate(jobs):
        if j not in seen:
            arrived(j, "a")
            seen.append(j)
        if j == rank:
            hq, hs = T.hq[:], T.hs[:]
        else:
            hq, hs = T.aq[:, col(j)], T["as"][:, col(j)]
        out = bank[:, BANK * i:BANK * i + n]
        t.matmul_mx(out, hq, hs, T.xq[:, c0:c0 + n], T.xs[:, c0:c0 + n], True, True).then_inc(sem["y%d" % k], 1)
        dst = T.yt[:, XC * j + c0:XC * j + c0 + n]
        if eng_name == "v":
            v.wait_ge(sem["y%d" % k], 1)
            v.tensor_copy(dst, out).then_inc(sem["c%d" % k], 1)
        else:
            a.wait_ge(sem["y%d" % k], 1)
            a.activation(dst, out, Copy).then_inc(sem["c%d" % k], 1)

    def store(q, j, waits, st):
        for k in waits:
            q.wait_ge(sem["c%d" % k], 1)
        q.dma_start(T.y[:, col(j, XC)], T.yt[:, col(j, XC)]).then_inc(st, 16)

    store(s, rank, [0], sem.st_sync)
    store(s, on, [1], sem.st_sync)
    store(s, off[0], [2, 3], sem.st_sync)
    store(a, off[1], [4, 5], sem.st_scal)
    s.wait_ge(sem.st_sync, 64)
    a.wait_ge(sem.st_scal, 16)
